import numpy as np
import ml_dtypes


def mxq(x, axis, fmt="e4m3"):
    dtype, down = {"e4m3": (ml_dtypes.float8_e4m3fn, 7), "e5m2": (ml_dtypes.float8_e5m2, 14)}[fmt]
    v = np.moveaxis(np.asarray(x, np.float32).astype(ml_dtypes.bfloat16).astype(np.float64), axis, -1)
    blocks = v.reshape(v.shape[:-1] + (-1, 32))
    amax = np.abs(blocks).max(-1, keepdims=True)
    byte = np.maximum(np.where(amax > 0, np.frexp(amax)[1] - 1 + 127, 0) - down, 1)
    scale = np.exp2(byte - 127.0)
    codes = (blocks / scale).astype(np.float32).astype(dtype).astype(np.float64)
    return np.moveaxis((codes * scale).reshape(v.shape), -1, axis)


WIDE = False


def mx_kscale(k):
    if not WIDE:
        return np.ones(k)
    levels = np.array([10, -10, 5, -5, 0])
    if k % 512:
        return np.exp2(np.random.permutation(np.resize(levels, k // 32))).repeat(32)
    a = np.empty((k // 512, 16))
    for p in range(k // 512):
        a[p, :8] = np.random.permutation(np.resize(levels, 8))
        for g in range(8):
            far = levels[np.abs(levels - a[p, g]) >= 10]
            a[p, g + 8] = far[np.random.randint(len(far))]
    return np.exp2(a.ravel()).repeat(32)


def f64(x):
    return np.asarray(x).astype(np.float64)


def striped(idx):
    return np.tile(idx.reshape(-1, 16).T, (8, 1)).astype(np.uint16)


def unstriped(offs):
    return offs[:16].T.reshape(-1).astype(np.int64)


def striped8(idx):
    return np.concatenate([x.reshape(-1, 16).T for x in idx]).astype(np.uint16)


def runs(offs, k):
    lists = np.stack([offs[16 * r : 16 * r + 16].T.reshape(-1) for r in range(8)]).astype(np.int64)
    return lists[np.arange(k) % 512 // 64]


def pack_weight(w):
    k, n = w.shape
    w = f64(np.asarray(w, np.float32).astype(ml_dtypes.bfloat16)).reshape(k // 32, 32, n)
    amax = np.abs(w).max(1)
    byte = np.clip(np.where(amax > 0, np.frexp(amax)[1] - 1 + 127 - 7, 1), 1, 254)
    scaled = (w * np.exp2(127.0 - byte)[:, None, :]).reshape(k, n).astype(np.float32)
    words = np.ascontiguousarray(scaled.reshape(k // 512, 128, 4, n).transpose(0, 1, 3, 2)).astype(ml_dtypes.float8_e4m3fn).view(np.uint8)
    return words, np.ascontiguousarray(byte.astype(np.uint8).reshape(k // 512, 16, n))


def unpack_weight(words, scales):
    g, p, n, _ = words.shape
    vals = np.ascontiguousarray(words).view(ml_dtypes.float8_e4m3fn).astype(np.float64) * np.repeat(np.exp2(scales.astype(np.float64) - 127.0), 8, axis=1)[..., None]
    return vals.transpose(0, 1, 3, 2).reshape(g * 512, n)


def sigmoid(v):
    return 1.0 / (1.0 + np.exp(-np.maximum(v, -700.0)))


K, T, S, H, C = 512, 2048, 512, 512, 512


def setup_inputs():
    n = np.random.standard_normal
    s = mx_kscale(K)[:, None]
    packed_xT = pack_weight(n((K, T)) * s)
    return {
        "x_words": packed_xT[0],
        "x_scales": packed_xT[1],
        "w1": (n((K, H)) / np.sqrt(K) / s).astype(np.float32),
        "gs": (np.random.uniform(0.5, 1.5, (K, 1)) / s).astype(np.float32),
        "offs": striped(np.random.permutation(T)[:S]),
        "n1": striped8(np.stack([np.random.permutation(S) for _ in range(8)])),
        "n2": striped8(np.stack([np.random.permutation(S) for _ in range(8)])),
        "ca": striped(np.random.permutation(T)[:C]),
        "cb": striped(np.random.permutation(T)[:C]),
        "n3": striped8(np.stack([np.random.permutation(S) for _ in range(8)])),
        "n4": striped8(np.stack([np.random.permutation(S) for _ in range(8)])),
        "n5": striped8(np.stack([np.random.permutation(S) for _ in range(8)])),
    }


def reference(x_words, x_scales, w1, gs, offs, n1, n2, ca, cb, n3, n4, n5):
    x_ca = unpack_weight(x_words, x_scales)[:, unstriped(ca)]
    xq = unpack_weight(x_words, x_scales)[:, unstriped(offs)]
    y = mxq(f64(w1), 0, "e4m3").T @ xq
    z = f64(gs) * (np.maximum(y * (sigmoid(y[np.arange(H)[:, None], runs(n1, H)])), y[np.arange(H)[:, None], runs(n2, H)]))
    zq = mxq(z, 0, "e4m3")
    a = 0.0625 * (x_ca.T @ zq)
    x_cb = unpack_weight(x_words, x_scales)[:, unstriped(cb)]
    b = 0.0625 * (x_cb.T @ zq)
    return np.maximum(np.minimum(a - (0.5 * (a[np.arange(C)[:, None], runs(n3, C)])), b[np.arange(C)[:, None], runs(n4, C)]), b[np.arange(C)[:, None], runs(n5, C)])

@@ -1,0 +1,250 @@
+from contextlib import ExitStack
+
+import concourse.mybir as mybir
+
+K, T, S, H, C = 512, 2048, 512, 512, 512
+FLOPS = 2 * K * H * S + 2 * (2 * K * C * S)
+
+F32 = mybir.dt.float32
+BF16 = mybir.dt.bfloat16
+I32 = mybir.dt.int32
+U32 = mybir.dt.uint32
+U16 = mybir.dt.uint16
+U8 = mybir.dt.uint8
+FP8X4 = mybir.dt.float8_e4m3fn_x4
+ALU = mybir.AluOpType
+ACT = mybir.ActivationFunctionType
+
+P = 128
+PACK = 4
+TILES = 4
+HALF = 256
+RUN = 8
+
+
+def tile_picked_ccmpclampbgmax_none_p_kernel(
+    tc, x_words, x_scales, w1, gs, offs, n1, n2, ca, cb, n3, n4, n5, out
+):
+    nc = tc.nc
+    with ExitStack() as ctx:
+        keep = ctx.enter_context(tc.tile_pool(name="keep", bufs=1))
+        psum = ctx.enter_context(tc.psum_pool(name="psum", bufs=1))
+
+        def list_tile(name):
+            return keep.tile([P, S // 16], U16, name=name)
+
+        def half_of(lst, h):
+            return lst[:, h * HALF // 16 : (h + 1) * HALF // 16]
+
+        def cols(h):
+            return slice(h * HALF, (h + 1) * HALF)
+
+        xs_win = keep.tile([P, T], U8, name="xs_win", align_bytes=64)
+        nc.vector.memset(xs_win[:].bitcast(I32), 0)
+        warm = keep.tile([P, 8], F32, name="warm")
+        warm_out = keep.tile([P, 8], F32, name="warm_out")
+        nc.vector.memset(warm[:], 0.0)
+        nc.scalar.activation(out=warm_out[:], in_=warm[:], func=ACT.Sigmoid)
+
+        offs_t, ca_t, cb_t = list_tile("offs_t"), list_tile("ca_t"), list_tile("cb_t")
+        w_raw = []
+        w_rows = w1.rearrange("(p j) c -> p j c", j=PACK)
+        for h in range(2):
+            w_half = keep.tile([P, PACK, HALF], F32, name="w_raw%d" % h)
+            nc.sync.dma_start(out=w_half[:], in_=w_rows[:, :, cols(h)])
+            w_raw.append(w_half)
+            if h == 0:
+                for q in range(4):
+                    nc.sync.dma_start(
+                        out=xs_win[32 * q : 32 * q + 4, :].bitcast(I32),
+                        in_=x_scales[0, 4 * q : 4 * q + 4, :].bitcast(I32),
+                    )
+                nc.sync.dma_start(offs_t[:], offs)
+        xw_win = keep.tile([P, T], I32, name="xw_win", align_bytes=64)
+        nc.sync.dma_start(out=xw_win[:], in_=x_words[0].rearrange("p n t -> p (n t)").bitcast(I32))
+        nc.sync.dma_start(ca_t[:], ca)
+        nc.sync.dma_start(cb_t[:], cb)
+        n_t = {}
+        for name, lst in (("n1", n1), ("n2", n2), ("n3", n3), ("n4", n4), ("n5", n5)):
+            n_t[name] = list_tile(name + "_t")
+            nc.sync.dma_start(n_t[name][:], lst)
+        gs_t = keep.tile([P, PACK], F32, name="gs_t")
+        nc.sync.dma_start(out=gs_t[:], in_=gs.rearrange("(p t) o -> p (t o)", t=PACK))
+
+        def gather_scales(offsets, width, name, tag):
+            got = keep.tile([P, width], U8, name=name, tag=tag, align_bytes=64)
+            nc.vector.tensor_copy(out=got[:], in_=xs_win[:].indirect(offsets))
+            return got
+
+        def deal_scales(dealt, got, g0):
+            groups = got.shape[1] // (TILES * RUN)
+            nc.vector.tensor_copy(
+                out=dealt[:].bitcast(I32).rearrange("p (t g w) -> p t g w", t=TILES, w=RUN // 4)[:, :, g0 : g0 + groups, :],
+                in_=got[:].bitcast(I32).rearrange("p (g t w) -> p t g w", t=TILES, w=RUN // 4),
+            )
+
+        def gather_words(lst, name, dealt, tag):
+            got = keep.tile([P, S], U32, name=name, tag=tag, align_bytes=64)
+            view = got[:].rearrange("p (t g r) -> p g t r", t=TILES, r=RUN) if dealt else got[:]
+            nc.vector.tensor_copy(out=view, in_=xw_win[:].bitcast(U32).indirect(lst[:]))
+            return got
+
+        x_s = gather_scales(offs_t[:], S, "x_s", "x_s")
+        ca_s = keep.tile([P, S], U8, name="ca_s", align_bytes=64)
+        cb_s = keep.tile([P, S], U8, name="cb_s", align_bytes=64)
+        deal_scales(ca_s, gather_scales(ca_t[:], S, "ca_s_raw", "ca_s_raw"), 0)
+        deal_scales(cb_s, gather_scales(half_of(cb_t, 0), HALF, "cb_s_raw0", "cb_s_raw0"), 0)
+
+        w_bf = keep.tile([P, TILES, P, PACK], BF16, name="w_bf", align_bytes=64)
+        for h in range(2):
+            m_cols = slice(h * P // 2, (h + 1) * P // 2)
+            nc.scalar.copy(
+                out=w_bf[:, :, m_cols, :].rearrange("p t m j -> p m j t"),
+                in_=w_raw[h][:].rearrange("p j (m t) -> p m j t", t=TILES),
+            )
+        x_w = gather_words(offs_t, "x_w", False, "x_w")
+        w_w = keep.tile([P, H], U32, name="w_w", align_bytes=64)
+        w_s = keep.tile([P, H], U8, name="w_s", align_bytes=64)
+        nc.vector.quantize_mx(
+            out=w_w[:].bitcast(FP8X4), scales=w_s[:], in_=w_bf[:].rearrange("p t m j -> p (t m j)")
+        )
+        ca_w = gather_words(ca_t, "ca_w", True, "ca_w")
+
+        y = []
+        for t in range(TILES):
+            bank = psum.tile([P, S], F32, name="y_ps%d" % t, tag="bank%d" % (4 + t))
+            tcols = slice(t * P, (t + 1) * P)
+            nc.tensor.matmul_mx(
+                out=bank[:], lhsT=w_w[:, tcols].bitcast(FP8X4), lhsT_scale=w_s[:, tcols],
+                rhs=x_w[:].bitcast(FP8X4), rhs_scale=x_s[:], start=True, stop=True,
+            )
+            y_t = keep.tile([P, S], F32, name="y%d" % t)
+            y.append((bank, y_t))
+
+        z_w = keep.tile([P, S], U32, name="z_w", align_bytes=64)
+        z_s = keep.tile([P, S], U8, name="z_s", align_bytes=64)
+        a_ps = [psum.tile([P, S], F32, name="a_ps%d" % t, tag="bank%d" % t) for t in range(TILES)]
+        a_win = [keep.tile([P, 2 * S], F32, name="a_win%d" % t) for t in range(TILES)]
+        b_win = [keep.tile([P, 2 * S], F32, name="b_win%d" % t) for t in range(TILES)]
+
+        def second(win, c):
+            return win[:, S + c.start : S + c.stop]
+
+        def product_a(t, h):
+            tcols = slice(t * P, (t + 1) * P)
+            nc.tensor.matmul_mx(
+                out=a_ps[t][:, cols(h)], lhsT=ca_w[:, tcols].bitcast(FP8X4), lhsT_scale=ca_s[:, tcols],
+                rhs=z_w[:, cols(h)].bitcast(FP8X4), rhs_scale=z_s[:, cols(h)], start=True, stop=True,
+            )
+
+        def copy_a(t, c):
+            nc.scalar.activation(out=a_win[t][:, c], in_=a_ps[t][:, c], func=ACT.Copy, scale=-0.03125)
+            nc.scalar.activation(out=second(b_win[t], c), in_=a_ps[t][:, c], func=ACT.Copy, scale=0.0625)
+
+        for h in range(2):
+            z_planes = keep.tile([P, TILES, HALF], BF16, name="z_planes%d" % h)
+            for t in range(TILES):
+                bank, y_t = y[t]
+                if h == 0:
+                    nc.scalar.activation(out=y_t[:], in_=bank[:], func=ACT.Copy)
+                sig = keep.tile([P, HALF], F32, name="sig%d_%d" % (t, h))
+                nc.scalar.activation(out=sig[:], in_=y_t[:].indirect(half_of(n_t["n1"], h)), func=ACT.Sigmoid)
+                other = keep.tile([P, HALF], F32, name="other%d_%d" % (t, h), tag="other%d_%d" % (t, h), align_bytes=64)
+                nc.vector.tensor_copy(out=other[:], in_=y_t[:].indirect(half_of(n_t["n2"], h)))
+                gated = keep.tile([P, HALF], F32, name="gated%d_%d" % (t, h))
+                nc.vector.tensor_tensor(out=gated[:], in0=y_t[:, cols(h)], in1=sig[:], op=ALU.mult)
+                larger = second(a_win[t], cols(h))
+                nc.vector.tensor_tensor(out=larger, in0=gated[:], in1=other[:], op=ALU.max)
+                nc.scalar.activation(out=z_planes[:, t, :], in_=larger, func=ACT.Copy, scale=gs_t[:, t : t + 1])
+            z_bf = keep.tile([P, HALF, PACK], BF16, name="z_bf%d" % h, tag="z_bf%d" % h, align_bytes=64)
+            if h == 1:
+                cb_s_raw1 = gather_scales(half_of(cb_t, 1), HALF, "cb_s_raw1", "other3_1")
+            weave = nc.scalar.copy if h == 0 else nc.vector.tensor_copy
+            weave(
+                out=z_bf[:].rearrange("p (c i) t -> p c t i", i=4),
+                in_=z_planes[:].rearrange("p t (c i) -> p c t i", i=4),
+            )
+            nc.vector.quantize_mx(
+                out=z_w[:, cols(h)].bitcast(FP8X4), scales=z_s[:, cols(h)], in_=z_bf[:].rearrange("p c t -> p (c t)")
+            )
+            if h == 0:
+                for t in range(TILES):
+                    product_a(t, 0)
+        copy_a(0, cols(0))
+        deal_scales(cb_s, cb_s_raw1, HALF // (TILES * RUN))
+        cb_w = gather_words(cb_t, "cb_w", True, "z_bf1")
+        b_ps = []
+        for t in range(TILES):
+            product_a(t, 1)
+        for t in range(TILES):
+            bank = psum.tile([P, S], F32, name="b_ps%d" % t, tag="bank%d" % (4 + t))
+            tcols = slice(t * P, (t + 1) * P)
+            nc.tensor.matmul_mx(
+                out=bank[:], lhsT=cb_w[:, tcols].bitcast(FP8X4), lhsT_scale=cb_s[:, tcols],
+                rhs=z_w[:].bitcast(FP8X4), rhs_scale=z_s[:], start=True, stop=True,
+            )
+            b_ps.append(bank)
+
+        out_rows = out.rearrange("(g t r) n -> t g r n", t=TILES, r=RUN)
+        whole = slice(0, S)
+        u = [keep.tile([P, S], F32, name="u%d" % t) for t in range(TILES)]
+        d4 = [keep.tile([P, S], F32, name="d4_%d" % t) for t in range(TILES)]
+        d5 = [keep.tile([P, S], F32, name="d5_%d" % t) for t in range(TILES)]
+        step = [keep.tile([P, S], F32, name="step%d" % t) for t in range(TILES)]
+        res = [keep.tile([P, S], F32, name="res%d" % t) for t in range(TILES)]
+
+        def entries(name, c):
+            return n_t[name][:, c.start // 16 : c.stop // 16]
+
+        def make_u(t, c):
+            nc.vector.tensor_tensor(
+                out=u[t][:, c], in0=a_win[t][:].indirect(entries("n3", c)), in1=second(b_win[t], c), op=ALU.add
+            )
+
+        def make_d(d, name, t, c):
+            nc.vector.tensor_tensor(
+                out=d[t][:, c], in0=b_win[t][:].indirect(entries(name, c)), in1=u[t][:, c], op=ALU.subtract
+            )
+
+        def make_step(t, c):
+            nc.vector.scalar_tensor_tensor(
+                out=step[t][:, c], in0=d4[t][:, c], scalar=0.0, in1=d5[t][:, c], op0=ALU.min, op1=ALU.max
+            )
+
+        def make_res(t, c):
+            nc.vector.tensor_tensor(out=res[t][:, c], in0=step[t][:, c], in1=u[t][:, c], op=ALU.add)
+
+        def copy_b(t):
+            nc.scalar.activation(out=b_win[t][:, whole], in_=b_ps[t][:], func=ACT.Copy, scale=0.0625)
+
+        copy_a(0, cols(1))
+        copy_a(1, whole)
+        for t in range(TILES):
+            copy_b(t)
+            if t + 2 < TILES:
+                copy_a(t + 2, whole)
+        make_u(0, cols(0))
+        make_u(0, cols(1))
+        make_u(1, whole)
+        make_d(d4, "n4", 0, whole)
+        for t in range(TILES - 1):
+            make_d(d5, "n5", t, whole)
+            if t + 2 < TILES:
+                make_u(t + 2, whole)
+                make_step(t, whole)
+                make_d(d4, "n4", t + 1, whole)
+            else:
+                make_d(d4, "n4", t + 1, cols(0))
+                make_step(t, whole)
+                make_d(d5, "n5", t + 1, cols(0))
+            make_res(t, whole)
+            nc.sync.dma_start(out=out_rows[t], in_=res[t][:])
+        last = TILES - 1
+        make_d(d4, "n4", last, cols(1))
+        make_step(last, cols(0))
+        make_d(d5, "n5", last, cols(1))
+        make_res(last, cols(0))
+        nc.sync.dma_start(out=out_rows[last][:, :, cols(0)], in_=res[last][:, cols(0)])
+        make_step(last, cols(1))
+        make_res(last, cols(1))
+        nc.sync.dma_start(out=out_rows[last][:, :, cols(1)], in_=res[last][:, cols(1)])

@@ -1,6 +1,7 @@
 from contextlib import ExitStack
 
 import concourse.mybir as mybir
+from concourse.masks import make_identity
 
 K, T, S, H, C = 512, 2048, 512, 512, 512
 FLOPS = 2 * K * H * S + 2 * (2 * K * C * S)
@@ -20,6 +21,7 @@ PACK = 4
 TILES = 4
 HALF = 256
 RUN = 8
+WEAVE_V = 176
 
 
 def tile_picked_ccmpclampbgmax_none_p_kernel(
@@ -41,28 +43,26 @@ def tile_picked_ccmpclampbgmax_none_p_kernel(
 
         xs_win = keep.tile([P, T], U8, name="xs_win", align_bytes=64)
         nc.vector.memset(xs_win[:].bitcast(I32), 0)
-        warm = keep.tile([P, 8], F32, name="warm")
+        warm = keep.tile([P, 8], F32, name="warm", tag="ident")
         warm_out = keep.tile([P, 8], F32, name="warm_out")
         nc.vector.memset(warm[:], 0.0)
         nc.scalar.activation(out=warm_out[:], in_=warm[:], func=ACT.Sigmoid)
+        ident = keep.tile([P, P], F32, name="ident", tag="ident")
+        make_identity(nc, ident[:])
 
         offs_t, ca_t, cb_t = list_tile("offs_t"), list_tile("ca_t"), list_tile("cb_t")
-        w_raw = []
         w_rows = w1.rearrange("(p j) c -> p j c", j=PACK)
-        for h in range(2):
-            w_half = keep.tile([P, PACK, HALF], F32, name="w_raw%d" % h)
-            nc.sync.dma_start(out=w_half[:], in_=w_rows[:, :, cols(h)])
-            w_raw.append(w_half)
-            if h == 0:
-                for q in range(4):
-                    nc.sync.dma_start(
-                        out=xs_win[32 * q : 32 * q + 4, :].bitcast(I32),
-                        in_=x_scales[0, 4 * q : 4 * q + 4, :].bitcast(I32),
-                    )
-                nc.sync.dma_start(offs_t[:], offs)
+        w_raw = [keep.tile([P, PACK, HALF], F32, name="w_raw%d" % h) for h in range(2)]
+        nc.sync.dma_start(out=w_raw[0][:], in_=w_rows[:, :, cols(0)])
+        for q in range(4):
+            nc.sync.dma_start(
+                out=xs_win[32 * q : 32 * q + 4, :].bitcast(I32), in_=x_scales[0, 4 * q : 4 * q + 4, :].bitcast(I32)
+            )
+        nc.sync.dma_start(offs_t[:], offs)
+        nc.sync.dma_start(ca_t[:], ca)
         xw_win = keep.tile([P, T], I32, name="xw_win", align_bytes=64)
         nc.sync.dma_start(out=xw_win[:], in_=x_words[0].rearrange("p n t -> p (n t)").bitcast(I32))
-        nc.sync.dma_start(ca_t[:], ca)
+        nc.sync.dma_start(out=w_raw[1][:], in_=w_rows[:, :, cols(1)])
         nc.sync.dma_start(cb_t[:], cb)
         n_t = {}
         for name, lst in (("n1", n1), ("n2", n2), ("n3", n3), ("n4", n4), ("n5", n5)):
@@ -93,9 +93,8 @@ def tile_picked_ccmpclampbgmax_none_p_kernel(
         ca_s = keep.tile([P, S], U8, name="ca_s", align_bytes=64)
         cb_s = keep.tile([P, S], U8, name="cb_s", align_bytes=64)
         deal_scales(ca_s, gather_scales(ca_t[:], S, "ca_s_raw", "ca_s_raw"), 0)
-        deal_scales(cb_s, gather_scales(half_of(cb_t, 0), HALF, "cb_s_raw0", "cb_s_raw0"), 0)
 
-        w_bf = keep.tile([P, TILES, P, PACK], BF16, name="w_bf", align_bytes=64)
+        w_bf = keep.tile([P, TILES, P, PACK], BF16, name="w_bf", tag="w_bf", align_bytes=64)
         for h in range(2):
             m_cols = slice(h * P // 2, (h + 1) * P // 2)
             nc.scalar.copy(
@@ -103,12 +102,15 @@ def tile_picked_ccmpclampbgmax_none_p_kernel(
                 in_=w_raw[h][:].rearrange("p j (m t) -> p m j t", t=TILES),
             )
         x_w = gather_words(offs_t, "x_w", False, "x_w")
+        ca_w = gather_words(ca_t, "ca_w", True, "ca_w")
         w_w = keep.tile([P, H], U32, name="w_w", align_bytes=64)
         w_s = keep.tile([P, H], U8, name="w_s", align_bytes=64)
-        nc.vector.quantize_mx(
-            out=w_w[:].bitcast(FP8X4), scales=w_s[:], in_=w_bf[:].rearrange("p t m j -> p (t m j)")
-        )
-        ca_w = gather_words(ca_t, "ca_w", True, "ca_w")
+        for h in range(2):
+            nc.vector.quantize_mx(
+                out=w_w[:, cols(h)].bitcast(FP8X4), scales=w_s[:, cols(h)],
+                in_=w_bf[:, 2 * h : 2 * h + 2].rearrange("p t m j -> p (t m j)"),
+            )
+        deal_scales(cb_s, gather_scales(cb_t[:], S, "cb_s_raw", "w_bf"), 0)
 
         y = []
         for t in range(TILES):
@@ -118,8 +120,7 @@ def tile_picked_ccmpclampbgmax_none_p_kernel(
                 out=bank[:], lhsT=w_w[:, tcols].bitcast(FP8X4), lhsT_scale=w_s[:, tcols],
                 rhs=x_w[:].bitcast(FP8X4), rhs_scale=x_s[:], start=True, stop=True,
             )
-            y_t = keep.tile([P, S], F32, name="y%d" % t)
-            y.append((bank, y_t))
+            y.append(bank)
 
         z_w = keep.tile([P, S], U32, name="z_w", align_bytes=64)
         z_s = keep.tile([P, S], U8, name="z_s", align_bytes=64)
@@ -130,71 +131,94 @@ def tile_picked_ccmpclampbgmax_none_p_kernel(
         def second(win, c):
             return win[:, S + c.start : S + c.stop]
 
-        def product_a(t, h):
-            tcols = slice(t * P, (t + 1) * P)
-            nc.tensor.matmul_mx(
-                out=a_ps[t][:, cols(h)], lhsT=ca_w[:, tcols].bitcast(FP8X4), lhsT_scale=ca_s[:, tcols],
-                rhs=z_w[:, cols(h)].bitcast(FP8X4), rhs_scale=z_s[:, cols(h)], start=True, stop=True,
-            )
-
         def copy_a(t, c):
             nc.scalar.activation(out=a_win[t][:, c], in_=a_ps[t][:, c], func=ACT.Copy, scale=-0.03125)
             nc.scalar.activation(out=second(b_win[t], c), in_=a_ps[t][:, c], func=ACT.Copy, scale=0.0625)
 
-        for h in range(2):
-            z_planes = keep.tile([P, TILES, HALF], BF16, name="z_planes%d" % h)
-            for t in range(TILES):
-                bank, y_t = y[t]
-                if h == 0:
-                    nc.scalar.activation(out=y_t[:], in_=bank[:], func=ACT.Copy)
-                sig = keep.tile([P, HALF], F32, name="sig%d_%d" % (t, h))
-                nc.scalar.activation(out=sig[:], in_=y_t[:].indirect(half_of(n_t["n1"], h)), func=ACT.Sigmoid)
-                other = keep.tile([P, HALF], F32, name="other%d_%d" % (t, h), tag="other%d_%d" % (t, h), align_bytes=64)
-                nc.vector.tensor_copy(out=other[:], in_=y_t[:].indirect(half_of(n_t["n2"], h)))
-                gated = keep.tile([P, HALF], F32, name="gated%d_%d" % (t, h))
-                nc.vector.tensor_tensor(out=gated[:], in0=y_t[:, cols(h)], in1=sig[:], op=ALU.mult)
-                larger = second(a_win[t], cols(h))
-                nc.vector.tensor_tensor(out=larger, in0=gated[:], in1=other[:], op=ALU.max)
-                nc.scalar.activation(out=z_planes[:, t, :], in_=larger, func=ACT.Copy, scale=gs_t[:, t : t + 1])
-            z_bf = keep.tile([P, HALF, PACK], BF16, name="z_bf%d" % h, tag="z_bf%d" % h, align_bytes=64)
-            if h == 1:
-                cb_s_raw1 = gather_scales(half_of(cb_t, 1), HALF, "cb_s_raw1", "other3_1")
-            weave = nc.scalar.copy if h == 0 else nc.vector.tensor_copy
-            weave(
-                out=z_bf[:].rearrange("p (c i) t -> p c t i", i=4),
-                in_=z_planes[:].rearrange("p t (c i) -> p c t i", i=4),
-            )
-            nc.vector.quantize_mx(
-                out=z_w[:, cols(h)].bitcast(FP8X4), scales=z_s[:, cols(h)], in_=z_bf[:].rearrange("p c t -> p (c t)")
-            )
-            if h == 0:
-                for t in range(TILES):
-                    product_a(t, 0)
-        copy_a(0, cols(0))
-        deal_scales(cb_s, cb_s_raw1, HALF // (TILES * RUN))
-        cb_w = gather_words(cb_t, "cb_w", True, "z_bf1")
-        b_ps = []
-        for t in range(TILES):
-            product_a(t, 1)
-        for t in range(TILES):
-            bank = psum.tile([P, S], F32, name="b_ps%d" % t, tag="bank%d" % (4 + t))
-            tcols = slice(t * P, (t + 1) * P)
-            nc.tensor.matmul_mx(
-                out=bank[:], lhsT=cb_w[:, tcols].bitcast(FP8X4), lhsT_scale=cb_s[:, tcols],
-                rhs=z_w[:].bitcast(FP8X4), rhs_scale=z_s[:], start=True, stop=True,
-            )
-            b_ps.append(bank)
-
-        out_rows = out.rearrange("(g t r) n -> t g r n", t=TILES, r=RUN)
         whole = slice(0, S)
-        u = [keep.tile([P, S], F32, name="u%d" % t) for t in range(TILES)]
-        d4 = [keep.tile([P, S], F32, name="d4_%d" % t) for t in range(TILES)]
-        d5 = [keep.tile([P, S], F32, name="d5_%d" % t) for t in range(TILES)]
-        step = [keep.tile([P, S], F32, name="step%d" % t) for t in range(TILES)]
-        res = [keep.tile([P, S], F32, name="res%d" % t) for t in range(TILES)]
 
         def entries(name, c):
             return n_t[name][:, c.start // 16 : c.stop // 16]
+
+        y_win = [keep.tile([P, S if t == 0 else 2 * S], F32, name="y_win%d" % t) for t in range(TILES)]
+        sig_last = keep.tile([P, S], F32, name="sig_last")
+        sig = [second(y_win[t + 1], whole) for t in range(TILES - 1)] + [sig_last[:]]
+        for t in range(TILES):
+            nc.scalar.activation(out=y_win[t][:, whole], in_=y[t][:], func=ACT.Copy)
+            for c in [cols(0), cols(1)] if t == 0 else [whole]:
+                nc.scalar.activation(out=sig[t][:, c], in_=y_win[t][:].indirect(entries("n1", c)), func=ACT.Sigmoid)
+
+        gated = [keep.tile([P, S], F32, name="gated%d" % t) for t in range(TILES)]
+        other = {}
+        z_planes = [keep.tile([P, TILES, HALF], BF16, name="z_planes%d" % h) for h in range(2)]
+
+        def fetch(t, h):
+            tag = "other%d_%d" % (t, h)
+            other[t, h] = keep.tile([P, HALF], F32, name=tag, tag=tag, align_bytes=64)
+            nc.vector.tensor_copy(out=other[t, h][:], in_=y_win[t][:].indirect(entries("n2", cols(h))))
+
+        def gate(t, h):
+            nc.vector.tensor_tensor(out=gated[t][:, cols(h)], in0=y_win[t][:, cols(h)], in1=sig[t][:, cols(h)], op=ALU.mult)
+
+        def larger(t, h):
+            dst = second(a_win[t], cols(h))
+            nc.vector.tensor_tensor(out=dst, in0=gated[t][:, cols(h)], in1=other[t, h][:], op=ALU.max)
+            nc.scalar.activation(out=z_planes[h][:, t, :], in_=dst, func=ACT.Copy, scale=gs_t[:, t : t + 1])
+
+        z_bf = [keep.tile([P, HALF, PACK], BF16, name="z_bf%d" % h, tag="z_bf%d" % h, align_bytes=64) for h in range(2)]
+
+        def weave(copy, h, c):
+            copy(
+                out=z_bf[h][:, c, :].rearrange("p (c i) t -> p c t i", i=4),
+                in_=z_planes[h][:, :, c].rearrange("p t (c i) -> p c t i", i=4),
+            )
+
+        def quantise_z(h):
+            nc.vector.quantize_mx(
+                out=z_w[:, cols(h)].bitcast(FP8X4), scales=z_s[:, cols(h)], in_=z_bf[h][:].rearrange("p c t -> p (c t)")
+            )
+
+        units = [(0, 0), (0, 1), (1, 0), (1, 1), (2, 0), (3, 0), (2, 1), (3, 1)]
+        for i, unit in enumerate(units):
+            fetch(*unit)
+            gate(*unit)
+            if i > 0:
+                larger(*units[i - 1])
+            if units[i - 1] == (TILES - 1, 0):
+                weave(nc.scalar.copy, 0, cols(0))
+        larger(*units[-1])
+        quantise_z(0)
+        weave(nc.vector.tensor_copy, 1, slice(0, WEAVE_V))
+        weave(nc.scalar.copy, 1, slice(WEAVE_V, HALF))
+        quantise_z(1)
+        cb_w = gather_words(cb_t, "cb_w", True, "z_bf1")
+
+        def product(dst, words, scales, t, c):
+            tcols = slice(t * P, (t + 1) * P)
+            nc.tensor.matmul_mx(
+                out=dst, lhsT=words[:, tcols].bitcast(FP8X4), lhsT_scale=scales[:, tcols],
+                rhs=z_w[:, c].bitcast(FP8X4), rhs_scale=z_s[:, c], start=True, stop=True,
+            )
+
+        a0_late = psum.tile([P, HALF], F32, name="a0_late", tag="bank7")
+        product(a_ps[0][:, cols(0)], ca_w, ca_s, 0, cols(0))
+        product(a0_late[:], ca_w, ca_s, 0, cols(1))
+        for t in range(1, TILES):
+            product(a_ps[t][:], ca_w, ca_s, t, whole)
+        nc.scalar.activation(out=a_win[0][:, cols(0)], in_=a_ps[0][:, cols(0)], func=ACT.Copy, scale=-0.03125)
+        nc.scalar.activation(out=second(b_win[0], cols(0)), in_=a_ps[0][:, cols(0)], func=ACT.Copy, scale=0.0625)
+        nc.scalar.activation(out=a_win[0][:, cols(1)], in_=a0_late[:], func=ACT.Copy, scale=-0.03125)
+        nc.scalar.activation(out=second(b_win[0], cols(1)), in_=a0_late[:], func=ACT.Copy, scale=0.0625)
+        b_ps = [psum.tile([P, S], F32, name="b_ps%d" % t, tag="bank%d" % (4 + t)) for t in range(TILES)]
+        for t in range(TILES):
+            product(b_ps[t][:], cb_w, cb_s, t, whole)
+
+        out_rows = out.rearrange("(g t r) n -> t g r n", t=TILES, r=RUN)
+        d4 = [keep.tile([P, S], F32, name="d4_%d" % t, tag="d4_%d" % t) for t in range(TILES)]
+        u = [keep.tile([P, S], F32, name="u%d" % t, tag="d4_1" if t == TILES - 1 else "u%d" % t) for t in range(TILES)]
+        d5 = [keep.tile([P, S], F32, name="d5_%d" % t) for t in range(TILES)]
+        step = [keep.tile([P, S], F32, name="step%d" % t) for t in range(TILES)]
+        res = [keep.tile([P, S], F32, name="res%d" % t) for t in range(TILES)]
 
         def make_u(t, c):
             nc.vector.tensor_tensor(
@@ -214,37 +238,70 @@ def tile_picked_ccmpclampbgmax_none_p_kernel(
         def make_res(t, c):
             nc.vector.tensor_tensor(out=res[t][:, c], in0=step[t][:, c], in1=u[t][:, c], op=ALU.add)
 
+        def add_by_transposes(t):
+            turned = keep.tile([P, S], F32, name="turned%d" % t)
+            blocks = [slice(b * P, (b + 1) * P) for b in range(HALF // P)]
+            for h in range(2):
+                turned_ps = psum.tile([P, HALF], F32, name="turned_ps%d_%d" % (t, h), tag="bank%d" % (4 * h + t))
+                for c in blocks:
+                    nc.tensor.matmul(
+                        turned_ps[:, c], u[t][:, cols(h)][:, c], ident[:], start=True, stop=False, is_transpose=True
+                    )
+                    nc.tensor.matmul(
+                        turned_ps[:, c], step[t][:, cols(h)][:, c], ident[:], start=False, stop=True, is_transpose=True
+                    )
+                nc.scalar.copy(out=turned[:, cols(h)], in_=turned_ps[:])
+            for h in range(2):
+                back_ps = psum.tile([P, HALF], F32, name="back_ps%d_%d" % (t, h), tag="bank%d" % (4 * h + t))
+                for c in blocks:
+                    nc.tensor.transpose(back_ps[:, c], turned[:, cols(h)][:, c], ident[:])
+                nc.scalar.copy(out=res[t][:, cols(h)], in_=back_ps[:])
+                nc.sync.dma_start(out=out_rows[t][:, :, cols(h)], in_=res[t][:, cols(h)])
+
         def copy_b(t):
             nc.scalar.activation(out=b_win[t][:, whole], in_=b_ps[t][:], func=ACT.Copy, scale=0.0625)
 
-        copy_a(0, cols(1))
         copy_a(1, whole)
         for t in range(TILES):
             copy_b(t)
             if t + 2 < TILES:
                 copy_a(t + 2, whole)
+
+        def finish(t):
+            make_step(t, whole)
+            add_by_transposes(t)
+
+        last = TILES - 1
         make_u(0, cols(0))
         make_u(0, cols(1))
         make_u(1, whole)
         make_d(d4, "n4", 0, whole)
-        for t in range(TILES - 1):
-            make_d(d5, "n5", t, whole)
-            if t + 2 < TILES:
-                make_u(t + 2, whole)
-                make_step(t, whole)
-                make_d(d4, "n4", t + 1, whole)
-            else:
-                make_d(d4, "n4", t + 1, cols(0))
-                make_step(t, whole)
-                make_d(d5, "n5", t + 1, cols(0))
-            make_res(t, whole)
-            nc.sync.dma_start(out=out_rows[t], in_=res[t][:])
-        last = TILES - 1
-        make_d(d4, "n4", last, cols(1))
-        make_step(last, cols(0))
-        make_d(d5, "n5", last, cols(1))
-        make_res(last, cols(0))
-        nc.sync.dma_start(out=out_rows[last][:, :, cols(0)], in_=res[last][:, cols(0)])
-        make_step(last, cols(1))
-        make_res(last, cols(1))
-        nc.sync.dma_start(out=out_rows[last][:, :, cols(1)], in_=res[last][:, cols(1)])
+        make_d(d5, "n5", 0, whole)
+        make_u(2, whole)
+        finish(0)
+        make_d(d4, "n4", 1, whole)
+        make_d(d5, "n5", 1, whole)
+        make_d(d4, "n4", 2, whole)
+        finish(1)
+        make_d(d5, "n5", 2, whole)
+        make_u(last, cols(0))
+        finish(2)
+        make_u(last, cols(1))
+        for h in range(2):
+            make_d(d4, "n4", last, cols(h))
+        for h in range(2):
+            nc.vector.scalar_tensor_tensor(
+                out=step[last][:, cols(h)], in0=d4[last][:, cols(h)], scalar=0.0, in1=u[last][:, cols(h)],
+                op0=ALU.min, op1=ALU.add,
+            )
+        for h in range(2):
+            nc.vector.tensor_tensor(
+                out=d5[last][:, cols(h)], in0=b_win[last][:].indirect(entries("n5", cols(h))),
+                in1=step[last][:, cols(h)], op=ALU.subtract,
+            )
+        for h in range(2):
+            nc.vector.scalar_tensor_tensor(
+                out=res[last][:, cols(h)], in0=d5[last][:, cols(h)], scalar=0.0, in1=step[last][:, cols(h)],
+                op0=ALU.max, op1=ALU.add,
+            )
+            nc.sync.dma_start(out=out_rows[last][:, :, cols(h)], in_=res[last][:, cols(h)])

@@ -43,12 +43,13 @@ def tile_picked_ccmpclampbgmax_none_p_kernel(
 
         xs_win = keep.tile([P, T], U8, name="xs_win", align_bytes=64)
         nc.vector.memset(xs_win[:].bitcast(I32), 0)
-        warm = keep.tile([P, 8], F32, name="warm", tag="ident")
+        ident = keep.tile([P, P], F32, name="ident")
+        nc.vector.memset(ident[:], 0.0)
+        make_identity(nc, ident[:], nomemset=True)
         warm_out = keep.tile([P, 8], F32, name="warm_out")
+        warm = keep.tile([P, 8], F32, name="warm")
         nc.vector.memset(warm[:], 0.0)
         nc.scalar.activation(out=warm_out[:], in_=warm[:], func=ACT.Sigmoid)
-        ident = keep.tile([P, P], F32, name="ident", tag="ident")
-        make_identity(nc, ident[:])
 
         offs_t, ca_t, cb_t = list_tile("offs_t"), list_tile("ca_t"), list_tile("cb_t")
         w_rows = w1.rearrange("(p j) c -> p j c", j=PACK)
@@ -90,9 +91,7 @@ def tile_picked_ccmpclampbgmax_none_p_kernel(
             return got
 
         x_s = gather_scales(offs_t[:], S, "x_s", "x_s")
-        ca_s = keep.tile([P, S], U8, name="ca_s", align_bytes=64)
-        cb_s = keep.tile([P, S], U8, name="cb_s", align_bytes=64)
-        deal_scales(ca_s, gather_scales(ca_t[:], S, "ca_s_raw", "ca_s_raw"), 0)
+        ca_s_raw = gather_scales(ca_t[:], S, "ca_s_raw", "ca_s_raw")
 
         w_bf = keep.tile([P, TILES, P, PACK], BF16, name="w_bf", tag="w_bf", align_bytes=64)
         for h in range(2):
@@ -110,7 +109,7 @@ def tile_picked_ccmpclampbgmax_none_p_kernel(
                 out=w_w[:, cols(h)].bitcast(FP8X4), scales=w_s[:, cols(h)],
                 in_=w_bf[:, 2 * h : 2 * h + 2].rearrange("p t m j -> p (t m j)"),
             )
-        deal_scales(cb_s, gather_scales(cb_t[:], S, "cb_s_raw", "w_bf"), 0)
+        cb_s_raw = gather_scales(cb_t[:], S, "cb_s_raw", "w_bf")
 
         y = []
         for t in range(TILES):
@@ -126,31 +125,35 @@ def tile_picked_ccmpclampbgmax_none_p_kernel(
         z_s = keep.tile([P, S], U8, name="z_s", align_bytes=64)
         a_ps = [psum.tile([P, S], F32, name="a_ps%d" % t, tag="bank%d" % t) for t in range(TILES)]
         a_win = [keep.tile([P, 2 * S], F32, name="a_win%d" % t) for t in range(TILES)]
-        b_win = [keep.tile([P, 2 * S], F32, name="b_win%d" % t) for t in range(TILES)]
+        b_win = [keep.tile([P, 2 * S if t < TILES - 1 else S], F32, name="b_win%d" % t) for t in range(TILES)]
+        a_last = keep.tile([P, S], F32, name="a_last")
+        a_full = [b_win[t][:, S:] for t in range(TILES - 1)] + [a_last[:]]
 
         def second(win, c):
             return win[:, S + c.start : S + c.stop]
 
         def copy_a(t, c):
             nc.scalar.activation(out=a_win[t][:, c], in_=a_ps[t][:, c], func=ACT.Copy, scale=-0.03125)
-            nc.scalar.activation(out=second(b_win[t], c), in_=a_ps[t][:, c], func=ACT.Copy, scale=0.0625)
+            nc.scalar.activation(out=a_full[t][:, c], in_=a_ps[t][:, c], func=ACT.Copy, scale=0.0625)
 
         whole = slice(0, S)
 
         def entries(name, c):
             return n_t[name][:, c.start // 16 : c.stop // 16]
 
-        y_win = [keep.tile([P, S if t == 0 else 2 * S], F32, name="y_win%d" % t) for t in range(TILES)]
-        sig_last = keep.tile([P, S], F32, name="sig_last")
-        sig = [second(y_win[t + 1], whole) for t in range(TILES - 1)] + [sig_last[:]]
-        for t in range(TILES):
-            nc.scalar.activation(out=y_win[t][:, whole], in_=y[t][:], func=ACT.Copy)
-            for c in [cols(0), cols(1)] if t == 0 else [whole]:
-                nc.scalar.activation(out=sig[t][:, c], in_=y_win[t][:].indirect(entries("n1", c)), func=ACT.Sigmoid)
+        units = [(0, 0), (0, 1), (1, 0), (2, 0), (3, 0), (1, 1), (2, 1), (3, 1)]
+        y_win = [keep.tile([P, S], F32, name="y_win%d" % t) for t in range(TILES)]
+        sig = [keep.tile([P, S], F32, name="sig%d" % t) for t in range(TILES)]
+        for t, h in units:
+            if h == 0:
+                nc.scalar.activation(out=y_win[t][:], in_=y[t][:], func=ACT.Copy)
+            nc.scalar.activation(
+                out=sig[t][:, cols(h)], in_=y_win[t][:].indirect(entries("n1", cols(h))), func=ACT.Sigmoid
+            )
 
         gated = [keep.tile([P, S], F32, name="gated%d" % t) for t in range(TILES)]
         other = {}
-        z_planes = [keep.tile([P, TILES, HALF], BF16, name="z_planes%d" % h) for h in range(2)]
+        z_planes = [keep.tile([P, TILES, HALF], BF16, name="z_planes%d" % h, tag="z_planes%d" % h, align_bytes=64) for h in range(2)]
 
         def fetch(t, h):
             tag = "other%d_%d" % (t, h)
@@ -178,7 +181,6 @@ def tile_picked_ccmpclampbgmax_none_p_kernel(
                 out=z_w[:, cols(h)].bitcast(FP8X4), scales=z_s[:, cols(h)], in_=z_bf[h][:].rearrange("p c t -> p (c t)")
             )
 
-        units = [(0, 0), (0, 1), (1, 0), (1, 1), (2, 0), (3, 0), (2, 1), (3, 1)]
         for i, unit in enumerate(units):
             fetch(*unit)
             gate(*unit)
@@ -187,9 +189,13 @@ def tile_picked_ccmpclampbgmax_none_p_kernel(
             if units[i - 1] == (TILES - 1, 0):
                 weave(nc.scalar.copy, 0, cols(0))
         larger(*units[-1])
+        ca_s = keep.tile([P, S], U8, name="ca_s", tag="other3_1", align_bytes=64)
+        deal_scales(ca_s, ca_s_raw, 0)
         quantise_z(0)
         weave(nc.vector.tensor_copy, 1, slice(0, WEAVE_V))
         weave(nc.scalar.copy, 1, slice(WEAVE_V, HALF))
+        cb_s = keep.tile([P, S], U8, name="cb_s", tag="z_planes1", align_bytes=64)
+        deal_scales(cb_s, cb_s_raw, 0)
         quantise_z(1)
         cb_w = gather_words(cb_t, "cb_w", True, "z_bf1")
 
@@ -206,9 +212,9 @@ def tile_picked_ccmpclampbgmax_none_p_kernel(
         for t in range(1, TILES):
             product(a_ps[t][:], ca_w, ca_s, t, whole)
         nc.scalar.activation(out=a_win[0][:, cols(0)], in_=a_ps[0][:, cols(0)], func=ACT.Copy, scale=-0.03125)
-        nc.scalar.activation(out=second(b_win[0], cols(0)), in_=a_ps[0][:, cols(0)], func=ACT.Copy, scale=0.0625)
+        nc.scalar.activation(out=a_full[0][:, cols(0)], in_=a_ps[0][:, cols(0)], func=ACT.Copy, scale=0.0625)
         nc.scalar.activation(out=a_win[0][:, cols(1)], in_=a0_late[:], func=ACT.Copy, scale=-0.03125)
-        nc.scalar.activation(out=second(b_win[0], cols(1)), in_=a0_late[:], func=ACT.Copy, scale=0.0625)
+        nc.scalar.activation(out=a_full[0][:, cols(1)], in_=a0_late[:], func=ACT.Copy, scale=0.0625)
         b_ps = [psum.tile([P, S], F32, name="b_ps%d" % t, tag="bank%d" % (4 + t)) for t in range(TILES)]
         for t in range(TILES):
             product(b_ps[t][:], cb_w, cb_s, t, whole)
@@ -222,7 +228,7 @@ def tile_picked_ccmpclampbgmax_none_p_kernel(
 
         def make_u(t, c):
             nc.vector.tensor_tensor(
-                out=u[t][:, c], in0=a_win[t][:].indirect(entries("n3", c)), in1=second(b_win[t], c), op=ALU.add
+                out=u[t][:, c], in0=a_win[t][:].indirect(entries("n3", c)), in1=a_full[t][:, c], op=ALU.add
             )
 
         def make_d(d, name, t, c):
@@ -294,14 +300,21 @@ def tile_picked_ccmpclampbgmax_none_p_kernel(
                 out=step[last][:, cols(h)], in0=d4[last][:, cols(h)], scalar=0.0, in1=u[last][:, cols(h)],
                 op0=ALU.min, op1=ALU.add,
             )
-        for h in range(2):
+
+        def fetch_last(c):
             nc.vector.tensor_tensor(
-                out=d5[last][:, cols(h)], in0=b_win[last][:].indirect(entries("n5", cols(h))),
-                in1=step[last][:, cols(h)], op=ALU.subtract,
+                out=d5[last][:, c], in0=b_win[last][:].indirect(entries("n5", c)), in1=step[last][:, c], op=ALU.subtract
             )
-        for h in range(2):
+
+        def finish_last(c):
             nc.vector.scalar_tensor_tensor(
-                out=res[last][:, cols(h)], in0=d5[last][:, cols(h)], scalar=0.0, in1=step[last][:, cols(h)],
-                op0=ALU.max, op1=ALU.add,
+                out=res[last][:, c], in0=d5[last][:, c], scalar=0.0, in1=step[last][:, c], op0=ALU.max, op1=ALU.add
             )
-            nc.sync.dma_start(out=out_rows[last][:, :, cols(h)], in_=res[last][:, cols(h)])
+            nc.sync.dma_start(out=out_rows[last][:, :, c], in_=res[last][:, c])
+
+        pieces = [slice(0, 256), slice(256, 384), slice(384, 512)]
+        for i, c in enumerate(pieces):
+            fetch_last(c)
+            if i > 0:
+                finish_last(pieces[i - 1])
+        finish_last(pieces[-1])

from contextlib import ExitStack

import concourse.mybir as mybir
from concourse.masks import make_identity

K, T, S, H, C = 512, 2048, 512, 512, 512
FLOPS = 2 * K * H * S + 2 * (2 * K * C * S)

F32 = mybir.dt.float32
BF16 = mybir.dt.bfloat16
I32 = mybir.dt.int32
U32 = mybir.dt.uint32
U16 = mybir.dt.uint16
U8 = mybir.dt.uint8
FP8X4 = mybir.dt.float8_e4m3fn_x4
ALU = mybir.AluOpType
ACT = mybir.ActivationFunctionType

P = 128
PACK = 4
TILES = 4
HALF = 256
RUN = 8
WEAVE_V = 176


def tile_picked_ccmpclampbgmax_none_p_kernel(
    tc, x_words, x_scales, w1, gs, offs, n1, n2, ca, cb, n3, n4, n5, out
):
    nc = tc.nc
    with ExitStack() as ctx:
        keep = ctx.enter_context(tc.tile_pool(name="keep", bufs=1))
        psum = ctx.enter_context(tc.psum_pool(name="psum", bufs=1))

        def list_tile(name):
            return keep.tile([P, S // 16], U16, name=name)

        def half_of(lst, h):
            return lst[:, h * HALF // 16 : (h + 1) * HALF // 16]

        def cols(h):
            return slice(h * HALF, (h + 1) * HALF)

        xs_win = keep.tile([P, T], U8, name="xs_win", align_bytes=64)
        nc.vector.memset(xs_win[:].bitcast(I32), 0)
        ident = keep.tile([P, P], F32, name="ident")
        nc.vector.memset(ident[:], 0.0)
        make_identity(nc, ident[:], nomemset=True)
        warm_out = keep.tile([P, 8], F32, name="warm_out")
        warm = keep.tile([P, 8], F32, name="warm")
        nc.vector.memset(warm[:], 0.0)
        nc.scalar.activation(out=warm_out[:], in_=warm[:], func=ACT.Sigmoid)

        offs_t, ca_t, cb_t = list_tile("offs_t"), list_tile("ca_t"), list_tile("cb_t")
        w_rows = w1.rearrange("(p j) c -> p j c", j=PACK)
        w_raw = [keep.tile([P, PACK, HALF], F32, name="w_raw%d" % h) for h in range(2)]
        nc.sync.dma_start(out=w_raw[0][:], in_=w_rows[:, :, cols(0)])
        for q in range(4):
            nc.sync.dma_start(
                out=xs_win[32 * q : 32 * q + 4, :].bitcast(I32), in_=x_scales[0, 4 * q : 4 * q + 4, :].bitcast(I32)
            )
        nc.sync.dma_start(offs_t[:], offs)
        nc.sync.dma_start(ca_t[:], ca)
        xw_win = keep.tile([P, T], I32, name="xw_win", align_bytes=64)
        nc.sync.dma_start(out=xw_win[:], in_=x_words[0].rearrange("p n t -> p (n t)").bitcast(I32))
        nc.sync.dma_start(out=w_raw[1][:], in_=w_rows[:, :, cols(1)])
        nc.sync.dma_start(cb_t[:], cb)
        n_t = {}
        for name, lst in (("n1", n1), ("n2", n2), ("n3", n3), ("n4", n4), ("n5", n5)):
            n_t[name] = list_tile(name + "_t")
            nc.sync.dma_start(n_t[name][:], lst)
        gs_t = keep.tile([P, PACK], F32, name="gs_t")
        nc.sync.dma_start(out=gs_t[:], in_=gs.rearrange("(p t) o -> p (t o)", t=PACK))

        def gather_scales(offsets, width, name, tag):
            got = keep.tile([P, width], U8, name=name, tag=tag, align_bytes=64)
            nc.vector.tensor_copy(out=got[:], in_=xs_win[:].indirect(offsets))
            return got

        def deal_scales(dealt, got, g0):
            groups = got.shape[1] // (TILES * RUN)
            nc.vector.tensor_copy(
                out=dealt[:].bitcast(I32).rearrange("p (t g w) -> p t g w", t=TILES, w=RUN // 4)[:, :, g0 : g0 + groups, :],
                in_=got[:].bitcast(I32).rearrange("p (g t w) -> p t g w", t=TILES, w=RUN // 4),
            )

        def gather_words(lst, name, dealt, tag):
            got = keep.tile([P, S], U32, name=name, tag=tag, align_bytes=64)
            view = got[:].rearrange("p (t g r) -> p g t r", t=TILES, r=RUN) if dealt else got[:]
            nc.vector.tensor_copy(out=view, in_=xw_win[:].bitcast(U32).indirect(lst[:]))
            return got

        x_s = gather_scales(offs_t[:], S, "x_s", "x_s")
        ca_s_raw = gather_scales(ca_t[:], S, "ca_s_raw", "ca_s_raw")

        w_bf = keep.tile([P, TILES, P, PACK], BF16, name="w_bf", tag="w_bf", align_bytes=64)
        for h in range(2):
            m_cols = slice(h * P // 2, (h + 1) * P // 2)
            nc.scalar.copy(
                out=w_bf[:, :, m_cols, :].rearrange("p t m j -> p m j t"),
                in_=w_raw[h][:].rearrange("p j (m t) -> p m j t", t=TILES),
            )
        x_w = gather_words(offs_t, "x_w", False, "x_w")
        ca_w = gather_words(ca_t, "ca_w", True, "ca_w")
        w_w = keep.tile([P, H], U32, name="w_w", align_bytes=64)
        w_s = keep.tile([P, H], U8, name="w_s", align_bytes=64)
        for h in range(2):
            nc.vector.quantize_mx(
                out=w_w[:, cols(h)].bitcast(FP8X4), scales=w_s[:, cols(h)],
                in_=w_bf[:, 2 * h : 2 * h + 2].rearrange("p t m j -> p (t m j)"),
            )
        cb_s_raw = gather_scales(cb_t[:], S, "cb_s_raw", "w_bf")

        y = []
        for t in range(TILES):
            bank = psum.tile([P, S], F32, name="y_ps%d" % t, tag="bank%d" % (4 + t))
            tcols = slice(t * P, (t + 1) * P)
            nc.tensor.matmul_mx(
                out=bank[:], lhsT=w_w[:, tcols].bitcast(FP8X4), lhsT_scale=w_s[:, tcols],
                rhs=x_w[:].bitcast(FP8X4), rhs_scale=x_s[:], start=True, stop=True,
            )
            y.append(bank)

        z_w = keep.tile([P, S], U32, name="z_w", align_bytes=64)
        z_s = keep.tile([P, S], U8, name="z_s", align_bytes=64)
        a_ps = [psum.tile([P, S], F32, name="a_ps%d" % t, tag="bank%d" % t) for t in range(TILES)]
        a_win = [keep.tile([P, 2 * S], F32, name="a_win%d" % t) for t in range(TILES)]
        b_win = [keep.tile([P, 2 * S if t < TILES - 1 else S], F32, name="b_win%d" % t) for t in range(TILES)]
        a_last = keep.tile([P, S], F32, name="a_last")
        a_full = [b_win[t][:, S:] for t in range(TILES - 1)] + [a_last[:]]

        def second(win, c):
            return win[:, S + c.start : S + c.stop]

        def copy_a(t, c):
            nc.scalar.activation(out=a_win[t][:, c], in_=a_ps[t][:, c], func=ACT.Copy, scale=-0.03125)
            nc.scalar.activation(out=a_full[t][:, c], in_=a_ps[t][:, c], func=ACT.Copy, scale=0.0625)

        whole = slice(0, S)

        def entries(name, c):
            return n_t[name][:, c.start // 16 : c.stop // 16]

        units = [(0, 0), (0, 1), (1, 0), (2, 0), (3, 0), (1, 1), (2, 1), (3, 1)]
        y_win = [keep.tile([P, S], F32, name="y_win%d" % t) for t in range(TILES)]
        sig = [keep.tile([P, S], F32, name="sig%d" % t) for t in range(TILES)]
        for t, h in units:
            if h == 0:
                nc.scalar.activation(out=y_win[t][:], in_=y[t][:], func=ACT.Copy)
            nc.scalar.activation(
                out=sig[t][:, cols(h)], in_=y_win[t][:].indirect(entries("n1", cols(h))), func=ACT.Sigmoid
            )

        gated = [keep.tile([P, S], F32, name="gated%d" % t) for t in range(TILES)]
        other = {}
        z_planes = [keep.tile([P, TILES, HALF], BF16, name="z_planes%d" % h, tag="z_planes%d" % h, align_bytes=64) for h in range(2)]

        def fetch(t, h):
            tag = "other%d_%d" % (t, h)
            other[t, h] = keep.tile([P, HALF], F32, name=tag, tag=tag, align_bytes=64)
            nc.vector.tensor_copy(out=other[t, h][:], in_=y_win[t][:].indirect(entries("n2", cols(h))))

        def gate(t, h):
            nc.vector.tensor_tensor(out=gated[t][:, cols(h)], in0=y_win[t][:, cols(h)], in1=sig[t][:, cols(h)], op=ALU.mult)

        def larger(t, h):
            dst = second(a_win[t], cols(h))
            nc.vector.tensor_tensor(out=dst, in0=gated[t][:, cols(h)], in1=other[t, h][:], op=ALU.max)
            nc.scalar.activation(out=z_planes[h][:, t, :], in_=dst, func=ACT.Copy, scale=gs_t[:, t : t + 1])

        z_bf = [keep.tile([P, HALF, PACK], BF16, name="z_bf%d" % h, tag="z_bf%d" % h, align_bytes=64) for h in range(2)]

        def weave(copy, h, c):
            copy(
                out=z_bf[h][:, c, :].rearrange("p (c i) t -> p c t i", i=4),
                in_=z_planes[h][:, :, c].rearrange("p t (c i) -> p c t i", i=4),
            )

        def quantise_z(h):
            nc.vector.quantize_mx(
                out=z_w[:, cols(h)].bitcast(FP8X4), scales=z_s[:, cols(h)], in_=z_bf[h][:].rearrange("p c t -> p (c t)")
            )

        for i, unit in enumerate(units):
            fetch(*unit)
            gate(*unit)
            if i > 0:
                larger(*units[i - 1])
            if units[i - 1] == (TILES - 1, 0):
                weave(nc.scalar.copy, 0, cols(0))
        larger(*units[-1])
        ca_s = keep.tile([P, S], U8, name="ca_s", tag="other3_1", align_bytes=64)
        deal_scales(ca_s, ca_s_raw, 0)
        quantise_z(0)
        weave(nc.vector.tensor_copy, 1, slice(0, WEAVE_V))
        weave(nc.scalar.copy, 1, slice(WEAVE_V, HALF))
        cb_s = keep.tile([P, S], U8, name="cb_s", tag="z_planes1", align_bytes=64)
        deal_scales(cb_s, cb_s_raw, 0)
        quantise_z(1)
        cb_w = gather_words(cb_t, "cb_w", True, "z_bf1")

        def product(dst, words, scales, t, c):
            tcols = slice(t * P, (t + 1) * P)
            nc.tensor.matmul_mx(
                out=dst, lhsT=words[:, tcols].bitcast(FP8X4), lhsT_scale=scales[:, tcols],
                rhs=z_w[:, c].bitcast(FP8X4), rhs_scale=z_s[:, c], start=True, stop=True,
            )

        a0_late = psum.tile([P, HALF], F32, name="a0_late", tag="bank7")
        product(a_ps[0][:, cols(0)], ca_w, ca_s, 0, cols(0))
        product(a0_late[:], ca_w, ca_s, 0, cols(1))
        for t in range(1, TILES):
            product(a_ps[t][:], ca_w, ca_s, t, whole)
        nc.scalar.activation(out=a_win[0][:, cols(0)], in_=a_ps[0][:, cols(0)], func=ACT.Copy, scale=-0.03125)
        nc.scalar.activation(out=a_full[0][:, cols(0)], in_=a_ps[0][:, cols(0)], func=ACT.Copy, scale=0.0625)
        nc.scalar.activation(out=a_win[0][:, cols(1)], in_=a0_late[:], func=ACT.Copy, scale=-0.03125)
        nc.scalar.activation(out=a_full[0][:, cols(1)], in_=a0_late[:], func=ACT.Copy, scale=0.0625)
        b_ps = [psum.tile([P, S], F32, name="b_ps%d" % t, tag="bank%d" % (4 + t)) for t in range(TILES)]
        for t in range(TILES):
            product(b_ps[t][:], cb_w, cb_s, t, whole)

        out_rows = out.rearrange("(g t r) n -> t g r n", t=TILES, r=RUN)
        d4 = [keep.tile([P, S], F32, name="d4_%d" % t, tag="d4_%d" % t) for t in range(TILES)]
        u = [keep.tile([P, S], F32, name="u%d" % t, tag="d4_1" if t == TILES - 1 else "u%d" % t) for t in range(TILES)]
        d5 = [keep.tile([P, S], F32, name="d5_%d" % t) for t in range(TILES)]
        step = [keep.tile([P, S], F32, name="step%d" % t) for t in range(TILES)]
        res = [keep.tile([P, S], F32, name="res%d" % t) for t in range(TILES)]

        def make_u(t, c):
            nc.vector.tensor_tensor(
                out=u[t][:, c], in0=a_win[t][:].indirect(entries("n3", c)), in1=a_full[t][:, c], op=ALU.add
            )

        def make_d(d, name, t, c):
            nc.vector.tensor_tensor(
                out=d[t][:, c], in0=b_win[t][:].indirect(entries(name, c)), in1=u[t][:, c], op=ALU.subtract
            )

        def make_step(t, c):
            nc.vector.scalar_tensor_tensor(
                out=step[t][:, c], in0=d4[t][:, c], scalar=0.0, in1=d5[t][:, c], op0=ALU.min, op1=ALU.max
            )

        def make_res(t, c):
            nc.vector.tensor_tensor(out=res[t][:, c], in0=step[t][:, c], in1=u[t][:, c], op=ALU.add)

        def add_by_transposes(t):
            turned = keep.tile([P, S], F32, name="turned%d" % t)
            blocks = [slice(b * P, (b + 1) * P) for b in range(HALF // P)]
            for h in range(2):
                turned_ps = psum.tile([P, HALF], F32, name="turned_ps%d_%d" % (t, h), tag="bank%d" % (4 * h + t))
                for c in blocks:
                    nc.tensor.matmul(
                        turned_ps[:, c], u[t][:, cols(h)][:, c], ident[:], start=True, stop=False, is_transpose=True
                    )
                    nc.tensor.matmul(
                        turned_ps[:, c], step[t][:, cols(h)][:, c], ident[:], start=False, stop=True, is_transpose=True
                    )
                nc.scalar.copy(out=turned[:, cols(h)], in_=turned_ps[:])
            for h in range(2):
                back_ps = psum.tile([P, HALF], F32, name="back_ps%d_%d" % (t, h), tag="bank%d" % (4 * h + t))
                for c in blocks:
                    nc.tensor.transpose(back_ps[:, c], turned[:, cols(h)][:, c], ident[:])
                nc.scalar.copy(out=res[t][:, cols(h)], in_=back_ps[:])
                nc.sync.dma_start(out=out_rows[t][:, :, cols(h)], in_=res[t][:, cols(h)])

        def copy_b(t):
            nc.scalar.activation(out=b_win[t][:, whole], in_=b_ps[t][:], func=ACT.Copy, scale=0.0625)

        copy_a(1, whole)
        for t in range(TILES):
            copy_b(t)
            if t + 2 < TILES:
                copy_a(t + 2, whole)

        def finish(t):
            make_step(t, whole)
            add_by_transposes(t)

        last = TILES - 1
        make_u(0, cols(0))
        make_u(0, cols(1))
        make_u(1, whole)
        make_d(d4, "n4", 0, whole)
        make_d(d5, "n5", 0, whole)
        make_u(2, whole)
        finish(0)
        make_d(d4, "n4", 1, whole)
        make_d(d5, "n5", 1, whole)
        make_d(d4, "n4", 2, whole)
        finish(1)
        make_d(d5, "n5", 2, whole)
        make_u(last, cols(0))
        finish(2)
        make_u(last, cols(1))
        for h in range(2):
            make_d(d4, "n4", last, cols(h))
        for h in range(2):
            nc.vector.scalar_tensor_tensor(
                out=step[last][:, cols(h)], in0=d4[last][:, cols(h)], scalar=0.0, in1=u[last][:, cols(h)],
                op0=ALU.min, op1=ALU.add,
            )

        def fetch_last(c):
            nc.vector.tensor_tensor(
                out=d5[last][:, c], in0=b_win[last][:].indirect(entries("n5", c)), in1=step[last][:, c], op=ALU.subtract
            )

        def finish_last(c):
            nc.vector.scalar_tensor_tensor(
                out=res[last][:, c], in0=d5[last][:, c], scalar=0.0, in1=step[last][:, c], op0=ALU.max, op1=ALU.add
            )
            nc.sync.dma_start(out=out_rows[last][:, :, c], in_=res[last][:, c])

        pieces = [slice(0, 256), slice(256, 384), slice(384, 512)]
        for i, c in enumerate(pieces):
            fetch_last(c)
            if i > 0:
                finish_last(pieces[i - 1])
        finish_last(pieces[-1])
